import numpy as np
import ml_dtypes


def mxq(x, axis, fmt="e4m3"):
    dtype, down = {"e4m3": (ml_dtypes.float8_e4m3fn, 7), "e5m2": (ml_dtypes.float8_e5m2, 14)}[fmt]
    v = np.moveaxis(np.asarray(x, np.float32).astype(ml_dtypes.bfloat16).astype(np.float64), axis, -1)
    blocks = v.reshape(v.shape[:-1] + (-1, 32))
    amax = np.abs(blocks).max(-1, keepdims=True)
    byte = np.maximum(np.where(amax > 0, np.frexp(amax)[1] - 1 + 127, 0) - down, 1)
    scale = np.exp2(byte - 127.0)
    codes = (blocks / scale).astype(np.float32).astype(dtype).astype(np.float64)
    return np.moveaxis((codes * scale).reshape(v.shape), -1, axis)


WIDE = False


def mx_kscale(k):
    if not WIDE:
        return np.ones(k)
    levels = np.array([10, -10, 5, -5, 0])
    if k % 512:
        return np.exp2(np.random.permutation(np.resize(levels, k // 32))).repeat(32)
    a = np.empty((k // 512, 16))
    for p in range(k // 512):
        a[p, :8] = np.random.permutation(np.resize(levels, 8))
        for g in range(8):
            far = levels[np.abs(levels - a[p, g]) >= 10]
            a[p, g + 8] = far[np.random.randint(len(far))]
    return np.exp2(a.ravel()).repeat(32)


def f64(x):
    return np.asarray(x).astype(np.float64)


def striped(idx):
    return np.tile(np.asarray(idx).reshape(-1, 16).T, (8, 1)).astype(np.uint16)


def unstriped(offs):
    return offs[:16].T.reshape(-1).astype(np.int64)


E2M1 = np.array([0.0, 0.5, 1.0, 1.5, 2.0, 3.0, 4.0, 6.0, -0.0, -0.5, -1.0, -1.5, -2.0, -3.0, -4.0, -6.0])


def pack_weight(w, fmt):
    k, n = w.shape
    w = f64(np.asarray(w, np.float32).astype(ml_dtypes.bfloat16)).reshape(k // 32, 32, n)
    amax = np.abs(w).max(1)
    if fmt == "e4m3":
        byte = np.frexp(amax)[1] - 1 + 127 - 7
    else:
        mant, ex = np.frexp(amax / 6.0)
        byte = np.where(mant > 0.5, ex, ex - 1) + 127
    byte = np.clip(np.where(amax > 0, byte, 1), 1, 254)
    scaled = (w * np.exp2(127.0 - byte)[:, None, :]).reshape(k, n).astype(np.float32)
    by_word = np.ascontiguousarray(scaled.reshape(k // 512, 128, 4, n).transpose(0, 1, 3, 2))
    if fmt == "e4m3":
        words = by_word.astype(ml_dtypes.float8_e4m3fn).view(np.uint8)
    else:
        c = by_word.astype(ml_dtypes.float4_e2m1fn).view(np.uint8) & 0xF
        words = (c[..., 0::2] | (c[..., 1::2] << 4)).reshape(k // 512, 128, 2 * n)
    return np.ascontiguousarray(words), np.ascontiguousarray(byte.astype(np.uint8).reshape(k // 512, 16, n))


def unpack_weight(words, scales, fmt):
    g, _, n = scales.shape
    words = np.ascontiguousarray(words).reshape(g, 128, n, -1)
    if fmt == "e4m3":
        vals = words.view(ml_dtypes.float8_e4m3fn).astype(np.float64)
    else:
        nib = np.empty((g, 128, n, 4), np.uint8)
        nib[..., 0::2] = words & 0xF
        nib[..., 1::2] = words >> 4
        vals = E2M1[nib]
    vals = vals * np.repeat(np.exp2(scales.astype(np.float64) - 127.0), 8, axis=1)[..., None]
    return vals.transpose(0, 1, 3, 2).reshape(g * 512, n)


def sigmoid(v):
    return 1.0 / (1.0 + np.exp(-v))


def bf(x):
    return np.asarray(x, np.float32).astype(ml_dtypes.bfloat16)


def planes(Y):
    r, m = Y.shape
    b = f64(bf(Y)).reshape(r // 32, 32, m)
    amax = np.abs(b).max(1)
    byte = np.clip(np.where(amax > 0, np.frexp(amax)[1] - 1 + 127 - 7, 1), 1, 254)
    codes = (b * np.exp2(127.0 - byte)[:, None, :]).reshape(r, m).astype(np.float32).astype(ml_dtypes.float8_e4m3fn).view(np.uint8)
    words = codes.reshape(r // 512, 128, 4, m).transpose(0, 1, 3, 2)
    return np.ascontiguousarray(words), np.ascontiguousarray(byte.astype(np.uint8).reshape(r // 512, 16, m))


K, T, J, R, V, N = 512, 2048, 512, 512, 1024, 512


def setup_inputs():
    n = np.random.standard_normal
    idx = np.random.permutation(T)[:J]
    idx2 = np.random.permutation(V)[:J]
    fk = mx_kscale(K)
    fr = mx_kscale(R)
    xtp = pack_weight(n((K, T)) / fk[:, None], "e2m1")
    wap = pack_weight(n((K, R)) * 1 / np.sqrt(K) * fk[:, None] * fr, "e4m3")
    wbp = pack_weight(n((R, N)) * 1 / np.sqrt(R) / fr[:, None], "e2m1")
    wyp = pack_weight(n((K, N)) * 1 / np.sqrt(K) * fk[:, None], "e4m3")
    return {
        "xt_words": xtp[0],
        "xt_scales": xtp[1],
        "wa_words": wap[0],
        "wa_scales": wap[1],
        "tb": (n((R, V))).astype(np.float32),
        "wb_words": wbp[0],
        "wb_scales": wbp[1],
        "wy_words": wyp[0],
        "wy_scales": wyp[1],
        "offs": striped(idx),
        "offs2": striped(idx2),
    }


def reference(xt_words, xt_scales, wa_words, wa_scales, tb, wb_words, wb_scales, wy_words, wy_scales, offs, offs2):
    idx = unstriped(offs)
    idx2 = unstriped(offs2)
    xtu = unpack_weight(xt_words, xt_scales, "e2m1")
    wau = unpack_weight(wa_words, wa_scales, "e4m3")
    wbu = unpack_weight(wb_words, wb_scales, "e2m1")
    wyu = unpack_weight(wy_words, wy_scales, "e4m3")
    xtidxg = xtu[:, idx]
    a = wau.T @ xtidxg
    hid = a * sigmoid(f64(tb)[:, idx2])
    hidq = mxq(hid, 0, "e4m3")
    y = wbu.T @ hidq + wyu.T @ xtidxg
    words, scales = planes(y)
    return y, words, scales

@@ -1,0 +1,202 @@
+from contextlib import ExitStack
+
+import concourse.mybir as mybir
+
+K, T, J, R, V, N = 512, 2048, 512, 512, 1024, 512
+FLOPS = 2 * J * (K * R + R * N + K * N)
+
+F32 = mybir.dt.float32
+BF16 = mybir.dt.bfloat16
+I32 = mybir.dt.int32
+U16 = mybir.dt.uint16
+U8 = mybir.dt.uint8
+FP8X4 = mybir.dt.float8_e4m3fn_x4
+FP4X4 = mybir.dt.float4_e2m1fn_x4
+SIGMOID = mybir.ActivationFunctionType.Sigmoid
+MULT = mybir.AluOpType.mult
+
+P = 128
+PACK = 4
+CHUNK = 128
+CHUNKS = J // CHUNK
+
+
+def load_scale_rows(queue, plane, rows):
+    for q in range(4):
+        queue.dma_start(out=plane[32 * q : 32 * q + 4, :].bitcast(I32), in_=rows[4 * q : 4 * q + 4, :].bitcast(I32))
+
+
+def deal(nc, dealt, raw, run):
+    nc.vector.tensor_copy(
+        out=dealt.rearrange("p (t c i) -> p c t i", t=PACK, i=run),
+        in_=raw.rearrange("p (c i t) -> p c t i", t=PACK, i=run),
+    )
+
+
+def tile_list_hidden_gated_by_table_pl_kernel(
+    tc, xt_words, xt_scales, wa_words, wa_scales, tb, wb_words, wb_scales, wy_words, wy_scales, offs, offs2,
+    out_0, out_1, out_2,
+):
+    nc = tc.nc
+    with ExitStack() as ctx:
+        sb = ctx.enter_context(tc.tile_pool(name="sb", bufs=1))
+        ps = ctx.enter_context(tc.psum_pool(name="ps", bufs=1))
+
+        def tile(name, shape, dtype):
+            return sb.tile(shape, dtype, name=name, align_bytes=64)
+
+        token_list = tile("token_list", [P, J // 16], U16)
+        gate_list = tile("gate_list", [P, J // 16], U16)
+        x_words = tile("x_words", [P, T], U16)
+        x_plane = tile("x_plane", [P, T], U8)
+        wa_raw = tile("wa_raw", [P, R], I32)
+        wy_raw = tile("wy_raw", [P, N], I32)
+        wb_raw = tile("wb_raw", [P, N], U16)
+        wa_plane_raw = tile("wa_plane_raw", [P, R], U8)
+        wy_plane_raw = tile("wy_plane_raw", [P, N], U8)
+        wb_plane_raw = tile("wb_plane_raw", [P, N], U8)
+        table = [tile("table%d" % t, [P, V], F32) for t in range(PACK)]
+        tb_rows = tb.rearrange("(p t) v -> t p v", t=PACK)
+
+        nc.vector.memset(x_plane[:].bitcast(I32), 0)
+        nc.gpsimd.memset(wa_plane_raw[:].bitcast(I32), 0)
+        nc.vector.memset(wy_plane_raw[:].bitcast(I32), 0)
+        nc.vector.memset(wb_plane_raw[:].bitcast(I32), 0)
+        warm_in = tile("warm_in", [P, 1], F32)
+        warm_out = tile("warm_out", [P, 1], F32)
+        nc.gpsimd.memset(warm_in[:], 0.0)
+        nc.scalar.activation(warm_out[:], warm_in[:], SIGMOID)
+
+        nc.sync.dma_start(token_list[:], offs)
+        nc.sync.dma_start(gate_list[:], offs2)
+        nc.sync.dma_start(out=x_words[:].bitcast(I32), in_=xt_words[0].bitcast(I32))
+        load_scale_rows(nc.sync, x_plane, xt_scales[0])
+        nc.sync.dma_start(out=table[0][:], in_=tb_rows[0])
+        nc.sync.dma_start(out=wa_raw[:], in_=wa_words[0].rearrange("p n t -> p (n t)").bitcast(I32))
+        load_scale_rows(nc.sync, wa_plane_raw, wa_scales[0])
+        nc.sync.dma_start(out=table[1][:], in_=tb_rows[1])
+        nc.sync.dma_start(out=wy_raw[:], in_=wy_words[0].rearrange("p n t -> p (n t)").bitcast(I32))
+        nc.sync.dma_start(out=wb_raw[:].bitcast(I32), in_=wb_words[0].bitcast(I32))
+        nc.sync.dma_start(out=table[2][:], in_=tb_rows[2])
+        load_scale_rows(nc.sync, wy_plane_raw, wy_scales[0])
+        nc.sync.dma_start(out=table[3][:], in_=tb_rows[3])
+        load_scale_rows(nc.sync, wb_plane_raw, wb_scales[0])
+
+        xg_words = tile("xg_words", [P, J], U16)
+        xg_plane = tile("xg_plane", [P, J], U8)
+        nc.vector.tensor_copy(xg_plane[:], x_plane[:].indirect(token_list[:]))
+        nc.vector.tensor_copy(xg_words[:], x_words[:].indirect(token_list[:]))
+
+        wa_codes = tile("wa_codes", [P, R], I32)
+        wa_plane = tile("wa_plane", [P, R], U8)
+        wy_codes = tile("wy_codes", [P, N], I32)
+        wy_plane = tile("wy_plane", [P, N], U8)
+        wb_codes = tile("wb_codes", [P, N], U16)
+        wb_plane = tile("wb_plane", [P, N], U8)
+        deal(nc, wa_codes[:], wa_raw[:], 2)
+        deal(nc, wa_plane[:], wa_plane_raw[:], 8)
+        deal(nc, wy_codes[:], wy_raw[:], 2)
+        deal(nc, wb_codes[:], wb_raw[:], 4)
+        deal(nc, wy_plane[:], wy_plane_raw[:], 8)
+        deal(nc, wb_plane[:], wb_plane_raw[:], 8)
+
+        def cols(c):
+            return slice(c * CHUNK, (c + 1) * CHUNK)
+
+        gate = [tile("gate%d" % c, [P, PACK, CHUNK], F32) for c in range(CHUNKS)]
+        for t in range(PACK):
+            for c in range(CHUNKS):
+                listed = gate_list[:, c * CHUNK // 16 : (c + 1) * CHUNK // 16]
+                nc.scalar.activation(gate[c][:, t, :], table[t][:].indirect(listed), SIGMOID)
+
+        a_bank = [ps.tile([P, PACK, CHUNK], F32, name="a_bank%d" % c) for c in range(CHUNKS)]
+        y_bank = [ps.tile([P, PACK, CHUNK], F32, name="y_bank%d" % c) for c in range(CHUNKS)]
+        for c in range(CHUNKS):
+            for t in range(PACK):
+                nc.tensor.matmul_mx(
+                    out=a_bank[c][:, t, :],
+                    lhsT=wa_codes[:, cols(t)].bitcast(FP8X4),
+                    lhsT_scale=wa_plane[:, cols(t)],
+                    rhs=xg_words[:, cols(c)].bitcast(FP4X4),
+                    rhs_scale=xg_plane[:, cols(c)],
+                    start=True,
+                    stop=True,
+                )
+        for c in range(CHUNKS):
+            for t in range(PACK):
+                nc.tensor.matmul_mx(
+                    out=y_bank[c][:, t, :],
+                    lhsT=wy_codes[:, cols(t)].bitcast(FP8X4),
+                    lhsT_scale=wy_plane[:, cols(t)],
+                    rhs=xg_words[:, cols(c)].bitcast(FP4X4),
+                    rhs_scale=xg_plane[:, cols(c)],
+                    start=(t == 0),
+                    stop=False,
+                )
+
+        hid = [tile("hid%d" % c, [P, CHUNK, PACK], BF16) for c in range(CHUNKS)]
+        hid_codes = [tile("hid_codes%d" % c, [P, CHUNK], I32) for c in range(CHUNKS)]
+        hid_plane = [tile("hid_plane%d" % c, [P, CHUNK], U8) for c in range(CHUNKS)]
+        y = [tile("y%d" % c, [P, PACK, CHUNK], F32) for c in range(CHUNKS)]
+        y_round = [tile("y_round%d" % c, [P, CHUNK, PACK], BF16) for c in range(CHUNKS)]
+        y_codes = tile("y_codes", [P, J], I32)
+        y_plane = tile("y_plane", [P, J], U8)
+        y_rows = out_0.rearrange("(p t) j -> p t j", t=PACK)
+        code_rows = out_1[0].rearrange("p c r -> p (c r)").bitcast(I32)
+
+        def gate_hidden(c):
+            nc.vector.tensor_tensor(
+                hid[c][:].rearrange("p (g i) t -> p g t i", i=2),
+                a_bank[c][:].rearrange("p t (g i) -> p g t i", i=2),
+                gate[c][:].rearrange("p t (g i) -> p g t i", i=2),
+                MULT,
+            )
+
+        def second_layer(c):
+            nc.vector.quantize_mx(
+                out=hid_codes[c][:].bitcast(FP8X4), scales=hid_plane[c][:], in_=hid[c][:].rearrange("p j t -> p (j t)")
+            )
+            for t in range(PACK):
+                nc.tensor.matmul_mx(
+                    out=y_bank[c][:, t, :],
+                    lhsT=wb_codes[:, cols(t)].bitcast(FP4X4),
+                    lhsT_scale=wb_plane[:, cols(t)],
+                    rhs=hid_codes[c][:].bitcast(FP8X4),
+                    rhs_scale=hid_plane[c][:],
+                    start=False,
+                    stop=(t == PACK - 1),
+                )
+            nc.scalar.copy(y[c][:], y_bank[c][:])
+            nc.sync.dma_start(out=y_rows[:, :, cols(c)], in_=y[c][:])
+
+        def round_y(c):
+            nc.vector.tensor_copy(
+                out=y_round[c][:].rearrange("p (g i) t -> p g t i", i=2),
+                in_=y[c][:].rearrange("p t (g i) -> p g t i", i=2),
+            )
+
+        def quantise_y(c):
+            nc.vector.quantize_mx(
+                out=y_codes[:, cols(c)].bitcast(FP8X4),
+                scales=y_plane[:, cols(c)],
+                in_=y_round[c][:].rearrange("p j t -> p (j t)"),
+            )
+            if c % 2 == 1:
+                half = slice((c - 1) * CHUNK, (c + 1) * CHUNK)
+                nc.sync.dma_start(out=code_rows[:, half], in_=y_codes[:, half])
+
+        gate_hidden(0)
+        for c in range(CHUNKS):
+            if c + 1 < CHUNKS:
+                gate_hidden(c + 1)
+            second_layer(c)
+        round_y(0)
+        for c in range(CHUNKS):
+            if c + 1 < CHUNKS:
+                round_y(c + 1)
+            quantise_y(c)
+        for q in range(4):
+            queue = nc.sync if q % 2 == 0 else nc.scalar
+            queue.dma_start(
+                out=out_2[0, 4 * q : 4 * q + 4, :].bitcast(I32), in_=y_plane[32 * q : 32 * q + 4, :].bitcast(I32)
+            )

@@ -19,11 +19,12 @@ P = 128
 PACK = 4
 CHUNK = 128
 CHUNKS = J // CHUNK
+HALF = J // 2
 
 
 def load_scale_rows(queue, plane, rows):
-    for q in range(4):
-        queue.dma_start(out=plane[32 * q : 32 * q + 4, :].bitcast(I32), in_=rows[4 * q : 4 * q + 4, :].bitcast(I32))
+    for r in range(4):
+        queue.dma_start(out=plane[r:P:32, :].bitcast(I32), in_=rows[r:16:4, :].bitcast(I32))
 
 
 def deal(nc, dealt, raw, run):
@@ -60,32 +61,32 @@ def tile_list_hidden_gated_by_table_pl_kernel(
 
         nc.vector.memset(x_plane[:].bitcast(I32), 0)
         nc.gpsimd.memset(wa_plane_raw[:].bitcast(I32), 0)
-        nc.vector.memset(wy_plane_raw[:].bitcast(I32), 0)
         nc.vector.memset(wb_plane_raw[:].bitcast(I32), 0)
+        nc.vector.memset(wy_plane_raw[:].bitcast(I32), 0)
         warm_in = tile("warm_in", [P, 1], F32)
         warm_out = tile("warm_out", [P, 1], F32)
         nc.gpsimd.memset(warm_in[:], 0.0)
         nc.scalar.activation(warm_out[:], warm_in[:], SIGMOID)
 
+        nc.sync.dma_start(out=x_words[:].bitcast(I32), in_=xt_words[0].bitcast(I32))
         nc.sync.dma_start(token_list[:], offs)
         nc.sync.dma_start(gate_list[:], offs2)
-        nc.sync.dma_start(out=x_words[:].bitcast(I32), in_=xt_words[0].bitcast(I32))
         load_scale_rows(nc.sync, x_plane, xt_scales[0])
         nc.sync.dma_start(out=table[0][:], in_=tb_rows[0])
         nc.sync.dma_start(out=wa_raw[:], in_=wa_words[0].rearrange("p n t -> p (n t)").bitcast(I32))
         load_scale_rows(nc.sync, wa_plane_raw, wa_scales[0])
         nc.sync.dma_start(out=table[1][:], in_=tb_rows[1])
-        nc.sync.dma_start(out=wy_raw[:], in_=wy_words[0].rearrange("p n t -> p (n t)").bitcast(I32))
         nc.sync.dma_start(out=wb_raw[:].bitcast(I32), in_=wb_words[0].bitcast(I32))
+        load_scale_rows(nc.sync, wb_plane_raw, wb_scales[0])
         nc.sync.dma_start(out=table[2][:], in_=tb_rows[2])
+        nc.sync.dma_start(out=wy_raw[:], in_=wy_words[0].rearrange("p n t -> p (n t)").bitcast(I32))
         load_scale_rows(nc.sync, wy_plane_raw, wy_scales[0])
         nc.sync.dma_start(out=table[3][:], in_=tb_rows[3])
-        load_scale_rows(nc.sync, wb_plane_raw, wb_scales[0])
 
         xg_words = tile("xg_words", [P, J], U16)
         xg_plane = tile("xg_plane", [P, J], U8)
-        nc.vector.tensor_copy(xg_plane[:], x_plane[:].indirect(token_list[:]))
         nc.vector.tensor_copy(xg_words[:], x_words[:].indirect(token_list[:]))
+        nc.vector.tensor_copy(xg_plane[:], x_plane[:].indirect(token_list[:]))
 
         wa_codes = tile("wa_codes", [P, R], I32)
         wa_plane = tile("wa_plane", [P, R], U8)
@@ -95,45 +96,38 @@ def tile_list_hidden_gated_by_table_pl_kernel(
         wb_plane = tile("wb_plane", [P, N], U8)
         deal(nc, wa_codes[:], wa_raw[:], 2)
         deal(nc, wa_plane[:], wa_plane_raw[:], 8)
-        deal(nc, wy_codes[:], wy_raw[:], 2)
         deal(nc, wb_codes[:], wb_raw[:], 4)
-        deal(nc, wy_plane[:], wy_plane_raw[:], 8)
         deal(nc, wb_plane[:], wb_plane_raw[:], 8)
 
         def cols(c):
             return slice(c * CHUNK, (c + 1) * CHUNK)
 
-        gate = [tile("gate%d" % c, [P, PACK, CHUNK], F32) for c in range(CHUNKS)]
-        for t in range(PACK):
+        gate_early = tile("gate_early", [P, 2, J], F32)
+        gate_late = [tile("gate_late%d" % c, [P, 2, CHUNK], F32) for c in range(CHUNKS)]
+        for e in range(2):
+            nc.scalar.activation(gate_early[:, e, :], table[e][:].indirect(gate_list[:]), SIGMOID)
+        for e in range(2):
             for c in range(CHUNKS):
                 listed = gate_list[:, c * CHUNK // 16 : (c + 1) * CHUNK // 16]
-                nc.scalar.activation(gate[c][:, t, :], table[t][:].indirect(listed), SIGMOID)
+                nc.scalar.activation(gate_late[c][:, e, :], table[2 + e][:].indirect(listed), SIGMOID)
 
-        a_bank = [ps.tile([P, PACK, CHUNK], F32, name="a_bank%d" % c) for c in range(CHUNKS)]
+        a_bank = [[ps.tile([P, 2, HALF], F32, name="a_bank%d%d" % (u, h)) for h in range(2)] for u in range(2)]
         y_bank = [ps.tile([P, PACK, CHUNK], F32, name="y_bank%d" % c) for c in range(CHUNKS)]
-        for c in range(CHUNKS):
-            for t in range(PACK):
-                nc.tensor.matmul_mx(
-                    out=a_bank[c][:, t, :],
-                    lhsT=wa_codes[:, cols(t)].bitcast(FP8X4),
-                    lhsT_scale=wa_plane[:, cols(t)],
-                    rhs=xg_words[:, cols(c)].bitcast(FP4X4),
-                    rhs_scale=xg_plane[:, cols(c)],
-                    start=True,
-                    stop=True,
-                )
-        for c in range(CHUNKS):
-            for t in range(PACK):
-                nc.tensor.matmul_mx(
-                    out=y_bank[c][:, t, :],
-                    lhsT=wy_codes[:, cols(t)].bitcast(FP8X4),
-                    lhsT_scale=wy_plane[:, cols(t)],
-                    rhs=xg_words[:, cols(c)].bitcast(FP4X4),
-                    rhs_scale=xg_plane[:, cols(c)],
-                    start=(t == 0),
-                    stop=False,
-                )
+        for u in range(2):
+            for h in range(2):
+                half = slice(h * HALF, (h + 1) * HALF)
+                for e in range(2):
+                    nc.tensor.matmul_mx(
+                        out=a_bank[u][h][:, e, :],
+                        lhsT=wa_codes[:, cols(2 * u + e)].bitcast(FP8X4),
+                        lhsT_scale=wa_plane[:, cols(2 * u + e)],
+                        rhs=xg_words[:, half].bitcast(FP4X4),
+                        rhs_scale=xg_plane[:, half],
+                        start=True,
+                        stop=True,
+                    )
 
+        pairs = [tile("pairs%d" % c, [P, 2, CHUNK, 2], BF16) for c in range(CHUNKS)]
         hid = [tile("hid%d" % c, [P, CHUNK, PACK], BF16) for c in range(CHUNKS)]
         hid_codes = [tile("hid_codes%d" % c, [P, CHUNK], I32) for c in range(CHUNKS)]
         hid_plane = [tile("hid_plane%d" % c, [P, CHUNK], U8) for c in range(CHUNKS)]
@@ -144,12 +138,18 @@ def tile_list_hidden_gated_by_table_pl_kernel(
         y_rows = out_0.rearrange("(p t) j -> p t j", t=PACK)
         code_rows = out_1[0].rearrange("p c r -> p (c r)").bitcast(I32)
 
-        def gate_hidden(c):
+        def gate_pair(u, c, gates):
             nc.vector.tensor_tensor(
-                hid[c][:].rearrange("p (g i) t -> p g t i", i=2),
-                a_bank[c][:].rearrange("p t (g i) -> p g t i", i=2),
-                gate[c][:].rearrange("p t (g i) -> p g t i", i=2),
+                pairs[c][:, u, :, :].rearrange("p (g i) e -> p g e i", i=4),
+                a_bank[u][c // 2][:, :, cols(c % 2)].rearrange("p e (g i) -> p g e i", i=4),
+                gates.rearrange("p e (g i) -> p g e i", i=4),
                 MULT,
+            )
+
+        def weave(c):
+            nc.vector.tensor_copy(
+                out=hid[c][:].rearrange("p j t -> p (j t)").bitcast(F32).rearrange("p (g i u) -> p g u i", i=2, u=2),
+                in_=pairs[c][:].rearrange("p u j e -> p (u j e)").bitcast(F32).rearrange("p (u g i) -> p g u i", i=2, u=2),
             )
 
         def second_layer(c):
@@ -166,13 +166,15 @@ def tile_list_hidden_gated_by_table_pl_kernel(
                     start=False,
                     stop=(t == PACK - 1),
                 )
+
+        def store_y(c):
             nc.scalar.copy(y[c][:], y_bank[c][:])
             nc.sync.dma_start(out=y_rows[:, :, cols(c)], in_=y[c][:])
 
-        def round_y(c):
+        def round_y(c, source):
             nc.vector.tensor_copy(
                 out=y_round[c][:].rearrange("p (g i) t -> p g t i", i=2),
-                in_=y[c][:].rearrange("p t (g i) -> p g t i", i=2),
+                in_=source[:].rearrange("p t (g i) -> p g t i", i=2),
             )
 
         def quantise_y(c):
@@ -181,22 +183,50 @@ def tile_list_hidden_gated_by_table_pl_kernel(
                 scales=y_plane[:, cols(c)],
                 in_=y_round[c][:].rearrange("p j t -> p (j t)"),
             )
-            if c % 2 == 1:
-                half = slice((c - 1) * CHUNK, (c + 1) * CHUNK)
-                nc.sync.dma_start(out=code_rows[:, half], in_=y_codes[:, half])
 
-        gate_hidden(0)
+        def store_codes(h):
+            half = slice(h * HALF, (h + 1) * HALF)
+            nc.sync.dma_start(out=code_rows[:, half], in_=y_codes[:, half])
+
         for c in range(CHUNKS):
-            if c + 1 < CHUNKS:
-                gate_hidden(c + 1)
-            second_layer(c)
-        round_y(0)
+            gate_pair(0, c, gate_early[:, :, cols(c)])
+
+        deal(nc, wy_codes[:], wy_raw[:], 2)
+        deal(nc, wy_plane[:], wy_plane_raw[:], 8)
         for c in range(CHUNKS):
-            if c + 1 < CHUNKS:
-                round_y(c + 1)
-            quantise_y(c)
-        for q in range(4):
-            queue = nc.sync if q % 2 == 0 else nc.scalar
-            queue.dma_start(
-                out=out_2[0, 4 * q : 4 * q + 4, :].bitcast(I32), in_=y_plane[32 * q : 32 * q + 4, :].bitcast(I32)
-            )
+            for t in range(PACK):
+                nc.tensor.matmul_mx(
+                    out=y_bank[c][:, t, :],
+                    lhsT=wy_codes[:, cols(t)].bitcast(FP8X4),
+                    lhsT_scale=wy_plane[:, cols(t)],
+                    rhs=xg_words[:, cols(c)].bitcast(FP4X4),
+                    rhs_scale=xg_plane[:, cols(c)],
+                    start=(t == 0),
+                    stop=False,
+                )
+
+        for h in range(2):
+            both = (2 * h, 2 * h + 1)
+            for c in both:
+                gate_pair(1, c, gate_late[c][:])
+            for c in both:
+                weave(c)
+            for c in both:
+                second_layer(c)
+        last = CHUNKS - 1
+        for c in range(last):
+            store_y(c)
+        round_y(0, y[0])
+        round_y(last, y_bank[last])
+        store_y(last)
+        quantise_y(0)
+        round_y(1, y[1])
+        quantise_y(last)
+        quantise_y(1)
+        store_codes(0)
+        round_y(2, y[2])
+        quantise_y(2)
+        store_codes(1)
+        for r in range(4):
+            queue = nc.sync if r % 2 == 0 else nc.scalar
+            queue.dma_start(out=out_2[0, r:16:4, :].bitcast(I32), in_=y_plane[r:P:32, :].bitcast(I32))

from contextlib import ExitStack

import concourse.mybir as mybir

K, T, J, R, V, N = 512, 2048, 512, 512, 1024, 512
FLOPS = 2 * J * (K * R + R * N + K * N)

F32 = mybir.dt.float32
BF16 = mybir.dt.bfloat16
I32 = mybir.dt.int32
U16 = mybir.dt.uint16
U8 = mybir.dt.uint8
FP8X4 = mybir.dt.float8_e4m3fn_x4
FP4X4 = mybir.dt.float4_e2m1fn_x4
SIGMOID = mybir.ActivationFunctionType.Sigmoid
MULT = mybir.AluOpType.mult

P = 128
PACK = 4
CHUNK = 128
CHUNKS = J // CHUNK
HALF = J // 2


def load_scale_rows(queue, plane, rows):
    for r in range(4):
        queue.dma_start(out=plane[r:P:32, :].bitcast(I32), in_=rows[r:16:4, :].bitcast(I32))


def deal(nc, dealt, raw, run):
    nc.vector.tensor_copy(
        out=dealt.rearrange("p (t c i) -> p c t i", t=PACK, i=run),
        in_=raw.rearrange("p (c i t) -> p c t i", t=PACK, i=run),
    )


def tile_list_hidden_gated_by_table_pl_kernel(
    tc, xt_words, xt_scales, wa_words, wa_scales, tb, wb_words, wb_scales, wy_words, wy_scales, offs, offs2,
    out_0, out_1, out_2,
):
    nc = tc.nc
    with ExitStack() as ctx:
        sb = ctx.enter_context(tc.tile_pool(name="sb", bufs=1))
        ps = ctx.enter_context(tc.psum_pool(name="ps", bufs=1))

        def tile(name, shape, dtype):
            return sb.tile(shape, dtype, name=name, align_bytes=64)

        token_list = tile("token_list", [P, J // 16], U16)
        gate_list = tile("gate_list", [P, J // 16], U16)
        x_words = tile("x_words", [P, T], U16)
        x_plane = tile("x_plane", [P, T], U8)
        wa_raw = tile("wa_raw", [P, R], I32)
        wy_raw = tile("wy_raw", [P, N], I32)
        wb_raw = tile("wb_raw", [P, N], U16)
        wa_plane_raw = tile("wa_plane_raw", [P, R], U8)
        wy_plane_raw = tile("wy_plane_raw", [P, N], U8)
        wb_plane_raw = tile("wb_plane_raw", [P, N], U8)
        table = [tile("table%d" % t, [P, V], F32) for t in range(PACK)]
        tb_rows = tb.rearrange("(p t) v -> t p v", t=PACK)

        nc.vector.memset(x_plane[:].bitcast(I32), 0)
        nc.gpsimd.memset(wa_plane_raw[:].bitcast(I32), 0)
        nc.vector.memset(wb_plane_raw[:].bitcast(I32), 0)
        nc.vector.memset(wy_plane_raw[:].bitcast(I32), 0)
        warm_in = tile("warm_in", [P, 1], F32)
        warm_out = tile("warm_out", [P, 1], F32)
        nc.gpsimd.memset(warm_in[:], 0.0)
        nc.scalar.activation(warm_out[:], warm_in[:], SIGMOID)

        nc.sync.dma_start(out=x_words[:].bitcast(I32), in_=xt_words[0].bitcast(I32))
        nc.sync.dma_start(token_list[:], offs)
        nc.sync.dma_start(gate_list[:], offs2)
        load_scale_rows(nc.sync, x_plane, xt_scales[0])
        nc.sync.dma_start(out=table[0][:], in_=tb_rows[0])
        nc.sync.dma_start(out=wa_raw[:], in_=wa_words[0].rearrange("p n t -> p (n t)").bitcast(I32))
        load_scale_rows(nc.sync, wa_plane_raw, wa_scales[0])
        nc.sync.dma_start(out=table[1][:], in_=tb_rows[1])
        nc.sync.dma_start(out=wb_raw[:].bitcast(I32), in_=wb_words[0].bitcast(I32))
        load_scale_rows(nc.sync, wb_plane_raw, wb_scales[0])
        nc.sync.dma_start(out=table[2][:], in_=tb_rows[2])
        nc.sync.dma_start(out=wy_raw[:], in_=wy_words[0].rearrange("p n t -> p (n t)").bitcast(I32))
        load_scale_rows(nc.sync, wy_plane_raw, wy_scales[0])
        nc.sync.dma_start(out=table[3][:], in_=tb_rows[3])

        xg_words = tile("xg_words", [P, J], U16)
        xg_plane = tile("xg_plane", [P, J], U8)
        nc.vector.tensor_copy(xg_words[:], x_words[:].indirect(token_list[:]))
        nc.vector.tensor_copy(xg_plane[:], x_plane[:].indirect(token_list[:]))

        wa_codes = tile("wa_codes", [P, R], I32)
        wa_plane = tile("wa_plane", [P, R], U8)
        wy_codes = tile("wy_codes", [P, N], I32)
        wy_plane = tile("wy_plane", [P, N], U8)
        wb_codes = tile("wb_codes", [P, N], U16)
        wb_plane = tile("wb_plane", [P, N], U8)
        deal(nc, wa_codes[:], wa_raw[:], 2)
        deal(nc, wa_plane[:], wa_plane_raw[:], 8)
        deal(nc, wb_codes[:], wb_raw[:], 4)
        deal(nc, wb_plane[:], wb_plane_raw[:], 8)

        def cols(c):
            return slice(c * CHUNK, (c + 1) * CHUNK)

        gate_early = tile("gate_early", [P, 2, J], F32)
        gate_late = [tile("gate_late%d" % c, [P, 2, CHUNK], F32) for c in range(CHUNKS)]
        for e in range(2):
            nc.scalar.activation(gate_early[:, e, :], table[e][:].indirect(gate_list[:]), SIGMOID)
        for e in range(2):
            for c in range(CHUNKS):
                listed = gate_list[:, c * CHUNK // 16 : (c + 1) * CHUNK // 16]
                nc.scalar.activation(gate_late[c][:, e, :], table[2 + e][:].indirect(listed), SIGMOID)

        a_bank = [[ps.tile([P, 2, HALF], F32, name="a_bank%d%d" % (u, h)) for h in range(2)] for u in range(2)]
        y_bank = [ps.tile([P, PACK, CHUNK], F32, name="y_bank%d" % c) for c in range(CHUNKS)]
        for u in range(2):
            for h in range(2):
                half = slice(h * HALF, (h + 1) * HALF)
                for e in range(2):
                    nc.tensor.matmul_mx(
                        out=a_bank[u][h][:, e, :],
                        lhsT=wa_codes[:, cols(2 * u + e)].bitcast(FP8X4),
                        lhsT_scale=wa_plane[:, cols(2 * u + e)],
                        rhs=xg_words[:, half].bitcast(FP4X4),
                        rhs_scale=xg_plane[:, half],
                        start=True,
                        stop=True,
                    )

        pairs = [tile("pairs%d" % c, [P, 2, CHUNK, 2], BF16) for c in range(CHUNKS)]
        hid = [tile("hid%d" % c, [P, CHUNK, PACK], BF16) for c in range(CHUNKS)]
        hid_codes = [tile("hid_codes%d" % c, [P, CHUNK], I32) for c in range(CHUNKS)]
        hid_plane = [tile("hid_plane%d" % c, [P, CHUNK], U8) for c in range(CHUNKS)]
        y = [tile("y%d" % c, [P, PACK, CHUNK], F32) for c in range(CHUNKS)]
        y_round = [tile("y_round%d" % c, [P, CHUNK, PACK], BF16) for c in range(CHUNKS)]
        y_codes = tile("y_codes", [P, J], I32)
        y_plane = tile("y_plane", [P, J], U8)
        y_rows = out_0.rearrange("(p t) j -> p t j", t=PACK)
        code_rows = out_1[0].rearrange("p c r -> p (c r)").bitcast(I32)

        def gate_pair(u, c, gates):
            nc.vector.tensor_tensor(
                pairs[c][:, u, :, :].rearrange("p (g i) e -> p g e i", i=4),
                a_bank[u][c // 2][:, :, cols(c % 2)].rearrange("p e (g i) -> p g e i", i=4),
                gates.rearrange("p e (g i) -> p g e i", i=4),
                MULT,
            )

        def weave(c):
            nc.vector.tensor_copy(
                out=hid[c][:].rearrange("p j t -> p (j t)").bitcast(F32).rearrange("p (g i u) -> p g u i", i=2, u=2),
                in_=pairs[c][:].rearrange("p u j e -> p (u j e)").bitcast(F32).rearrange("p (u g i) -> p g u i", i=2, u=2),
            )

        def second_layer(c):
            nc.vector.quantize_mx(
                out=hid_codes[c][:].bitcast(FP8X4), scales=hid_plane[c][:], in_=hid[c][:].rearrange("p j t -> p (j t)")
            )
            for t in range(PACK):
                nc.tensor.matmul_mx(
                    out=y_bank[c][:, t, :],
                    lhsT=wb_codes[:, cols(t)].bitcast(FP4X4),
                    lhsT_scale=wb_plane[:, cols(t)],
                    rhs=hid_codes[c][:].bitcast(FP8X4),
                    rhs_scale=hid_plane[c][:],
                    start=False,
                    stop=(t == PACK - 1),
                )

        def store_y(c):
            nc.scalar.copy(y[c][:], y_bank[c][:])
            nc.sync.dma_start(out=y_rows[:, :, cols(c)], in_=y[c][:])

        def round_y(c, source):
            nc.vector.tensor_copy(
                out=y_round[c][:].rearrange("p (g i) t -> p g t i", i=2),
                in_=source[:].rearrange("p t (g i) -> p g t i", i=2),
            )

        def quantise_y(c):
            nc.vector.quantize_mx(
                out=y_codes[:, cols(c)].bitcast(FP8X4),
                scales=y_plane[:, cols(c)],
                in_=y_round[c][:].rearrange("p j t -> p (j t)"),
            )

        def store_codes(h):
            half = slice(h * HALF, (h + 1) * HALF)
            nc.sync.dma_start(out=code_rows[:, half], in_=y_codes[:, half])

        for c in range(CHUNKS):
            gate_pair(0, c, gate_early[:, :, cols(c)])

        deal(nc, wy_codes[:], wy_raw[:], 2)
        deal(nc, wy_plane[:], wy_plane_raw[:], 8)
        for c in range(CHUNKS):
            for t in range(PACK):
                nc.tensor.matmul_mx(
                    out=y_bank[c][:, t, :],
                    lhsT=wy_codes[:, cols(t)].bitcast(FP8X4),
                    lhsT_scale=wy_plane[:, cols(t)],
                    rhs=xg_words[:, cols(c)].bitcast(FP4X4),
                    rhs_scale=xg_plane[:, cols(c)],
                    start=(t == 0),
                    stop=False,
                )

        for h in range(2):
            both = (2 * h, 2 * h + 1)
            for c in both:
                gate_pair(1, c, gate_late[c][:])
            for c in both:
                weave(c)
            for c in both:
                second_layer(c)
        last = CHUNKS - 1
        for c in range(last):
            store_y(c)
        round_y(0, y[0])
        round_y(last, y_bank[last])
        store_y(last)
        quantise_y(0)
        round_y(1, y[1])
        quantise_y(last)
        quantise_y(1)
        store_codes(0)
        round_y(2, y[2])
        quantise_y(2)
        store_codes(1)
        for r in range(4):
            queue = nc.sync if r % 2 == 0 else nc.scalar
            queue.dma_start(out=out_2[0, r:16:4, :].bitcast(I32), in_=y_plane[r:P:32, :].bitcast(I32))
